import numpy as np
import ml_dtypes


def mxq(x, axis, fmt="e4m3"):
    dtype, down = {"e4m3": (ml_dtypes.float8_e4m3fn, 7), "e5m2": (ml_dtypes.float8_e5m2, 14)}[fmt]
    v = np.moveaxis(np.asarray(x, np.float32).astype(ml_dtypes.bfloat16).astype(np.float64), axis, -1)
    blocks = v.reshape(v.shape[:-1] + (-1, 32))
    amax = np.abs(blocks).max(-1, keepdims=True)
    byte = np.maximum(np.where(amax > 0, np.frexp(amax)[1] - 1 + 127, 0) - down, 1)
    scale = np.exp2(byte - 127.0)
    codes = (blocks / scale).astype(np.float32).astype(dtype).astype(np.float64)
    return np.moveaxis((codes * scale).reshape(v.shape), -1, axis)


WIDE = False


def mx_kscale(k):
    if not WIDE:
        return np.ones(k)
    levels = np.array([10, -10, 5, -5, 0])
    if k % 512:
        return np.exp2(np.random.permutation(np.resize(levels, k // 32))).repeat(32)
    a = np.empty((k // 512, 16))
    for p in range(k // 512):
        a[p, :8] = np.random.permutation(np.resize(levels, 8))
        for g in range(8):
            far = levels[np.abs(levels - a[p, g]) >= 10]
            a[p, g + 8] = far[np.random.randint(len(far))]
    return np.exp2(a.ravel()).repeat(32)


def f64(x):
    return np.asarray(x).astype(np.float64)


def striped(idx):
    return np.tile(idx.reshape(-1, 16).T, (8, 1)).astype(np.uint16)


def unstriped(offs):
    return offs[:16].T.reshape(-1).astype(np.int64)


E2M1 = np.array([0.0, 0.5, 1.0, 1.5, 2.0, 3.0, 4.0, 6.0, -0.0, -0.5, -1.0, -1.5, -2.0, -3.0, -4.0, -6.0])


def pack_weight(w, fmt):
    k, n = w.shape
    w = f64(np.asarray(w, np.float32).astype(ml_dtypes.bfloat16)).reshape(k // 32, 32, n)
    amax = np.abs(w).max(1)
    if fmt == "e4m3":
        byte = np.frexp(amax)[1] - 1 + 127 - 7
    else:
        mant, ex = np.frexp(amax / 6.0)
        byte = np.where(mant > 0.5, ex, ex - 1) + 127
    byte = np.clip(np.where(amax > 0, byte, 1), 1, 254)
    scaled = (w * np.exp2(127.0 - byte)[:, None, :]).reshape(k, n).astype(np.float32)
    by_word = np.ascontiguousarray(scaled.reshape(k // 512, 128, 4, n).transpose(0, 1, 3, 2))
    if fmt == "e4m3":
        words = by_word.astype(ml_dtypes.float8_e4m3fn).view(np.uint8)
    else:
        c = by_word.astype(ml_dtypes.float4_e2m1fn).view(np.uint8) & 0xF
        words = (c[..., 0::2] | (c[..., 1::2] << 4)).reshape(k // 512, 128, 2 * n)
    return np.ascontiguousarray(words), np.ascontiguousarray(byte.astype(np.uint8).reshape(k // 512, 16, n))


def unpack_weight(words, scales, fmt):
    g, _, n = scales.shape
    words = np.ascontiguousarray(words).reshape(g, 128, n, -1)
    if fmt == "e4m3":
        vals = words.view(ml_dtypes.float8_e4m3fn).astype(np.float64)
    else:
        nib = np.empty((g, 128, n, 4), np.uint8)
        nib[..., 0::2] = words & 0xF
        nib[..., 1::2] = words >> 4
        vals = E2M1[nib]
    vals = vals * np.repeat(np.exp2(scales.astype(np.float64) - 127.0), 8, axis=1)[..., None]
    return vals.transpose(0, 1, 3, 2).reshape(g * 512, n)


def gelu(v):
    return 0.5 * v * (1.0 + np.tanh(np.sqrt(2.0 / np.pi) * (v + 0.044715 * v**3)))


def striped8(idx):
    return np.concatenate([v.reshape(-1, 16).T for v in idx]).astype(np.uint16)


def unstriped8(offs):
    return np.stack([offs[16 * g:16 * g + 16].T.reshape(-1) for g in range(8)]).astype(np.int64)


def heads(h, wgt, idx8):
    r = np.arange(h.shape[0])
    return wgt[r // 4 % 128] * h[r[:, None], idx8[r % 512 // 64]]


def put_heads(h, wgs, idx8, t2):
    r = np.arange(h.shape[0])
    page = np.zeros((h.shape[0], t2))
    page[r[:, None], idx8[r % 512 // 64]] = wgs[r // 4 % 128] * h
    return page


K, H, N, T, S, T2, P = 1536, 1024, 384, 4096, 1024, 2048, 1024

def setup_inputs():
    n = np.random.standard_normal
    s = mx_kscale(K)[:, None]
    u = mx_kscale(H)[:, None]
    d = {}
    d["tab_words"], d["tab_scales"] = pack_weight(n((K, T)) * s, "e4m3")
    d["offs"] = striped(np.random.permutation(T)[:S])
    d["w1"] = (1.4 * n((K, H)) / K**0.5 / s).astype(np.float32)
    d["b1"] = (0.6 * n(H)).astype(np.float32)
    d["gain"] = (np.exp(0.3 * n(H)) * u[:, 0]).astype(np.float32)
    d["offs2"] = striped8(np.stack([np.random.permutation(T2)[:S] for _ in range(8)]))
    d["wgs"] = np.repeat(np.random.uniform(0.5, 2.0, (8, S)), 16, axis=0).astype(np.float32)
    d["offs3"] = striped8(np.stack([np.random.permutation(T2)[:P] for _ in range(8)]))
    d["wgt"] = np.repeat(np.random.uniform(0.5, 2.0, (8, P)), 16, axis=0).astype(np.float32)
    d["room"] = (0.7 * n((H, P)) * u).astype(np.float32)
    d["w4_words"], d["w4_scales"] = pack_weight(n((H, N)) / H**0.5 / u, "e2m1")
    d["b2"] = (0.4 * n(N)).astype(np.float32)
    return d

def reference(tab_words, tab_scales, offs, w1, b1, gain, offs2, wgs, offs3, wgt, room, w4_words, w4_scales, b2):
    v = unpack_weight(tab_words, tab_scales, "e4m3")[:, unstriped(offs)]
    resp = mxq(f64(w1), 0, "e4m3").T @ v
    h = f64(gain)[:, None] * np.tanh(resp + f64(b1)[:, None])
    page = put_heads(h, f64(wgs), unstriped8(offs2), T2)
    x = heads(page, f64(wgt), unstriped8(offs3))
    z = x + f64(room)
    w4 = unpack_weight(w4_words, w4_scales, "e2m1")
    y = w4.T @ mxq(z, 0, "e4m3")
    return y + f64(b2)[:, None]

@@ -1,0 +1,321 @@
+from contextlib import ExitStack
+
+import concourse.mybir as mybir
+from concourse.masks import make_identity
+
+K, H, N, T, S, T2, M = 1536, 1024, 384, 4096, 1024, 2048, 1024
+FLOPS = 2 * K * H * S + 2 * H * N * M
+
+F32 = mybir.dt.float32
+BF16 = mybir.dt.bfloat16
+I32 = mybir.dt.int32
+U32 = mybir.dt.uint32
+U16 = mybir.dt.uint16
+U8 = mybir.dt.uint8
+FP8X4 = mybir.dt.float8_e4m3fn_x4
+FP4X4 = mybir.dt.float4_e2m1fn_x4
+MULT = mybir.AluOpType.mult
+ADD = mybir.AluOpType.add
+ACT = mybir.ActivationFunctionType
+
+P = 128
+PACK = 4
+PASS = P * PACK
+K_PASSES = K // PASS
+H_PASSES = H // PASS
+BANK = 512
+STRIPE = 16
+LAST_PIECES = (256, 256, 256, 128, 128)
+
+
+def tile_list_organ_pipe_voicing_kernel(
+    tc, tab_words, tab_scales, offs, w1, b1, gain, offs2, wgs, offs3, wgt, room, w4_words, w4_scales, b2, out
+):
+    nc = tc.nc
+
+    def entries(list_tile, lo, hi):
+        return list_tile[:, lo // STRIPE : hi // STRIPE]
+
+    with ExitStack() as ctx:
+        keep = ctx.enter_context(tc.tile_pool(name="keep", bufs=1))
+        ring = ctx.enter_context(tc.tile_pool(name="ring", bufs=1))
+        psum = ctx.enter_context(tc.psum_pool(name="psum", bufs=1))
+
+        offs_t = keep.tile([P, S // STRIPE], U16, name="offs_t")
+        offs2_t = keep.tile([P, S // STRIPE], U16, name="offs2_t")
+        offs3_t = keep.tile([P, M // STRIPE], U16, name="offs3_t")
+
+        tab_planes = keep.tile([P, T], U8, name="tab_planes", align_bytes=64)
+        w4_planes = keep.tile([P, H_PASSES, N], U8, name="w4_planes", align_bytes=64)
+        nc.gpsimd.memset(tab_planes[:].bitcast(I32), 0)
+        warm = keep.tile([P, 2], F32, name="warm")
+        nc.vector.memset(warm[:, 0:1], 0.0)
+        nc.scalar.activation(warm[:, 1:2], warm[:, 0:1], ACT.Tanh)
+        b1_t = keep.tile([P, H_PASSES, PACK], F32, name="b1_t")
+        gain_t = keep.tile([P, H_PASSES, PACK], F32, name="gain_t")
+        ident = keep.tile([P, P], F32, name="ident")
+        make_identity(nc, ident[:])
+
+        pages = [keep.tile([P, T2], F32, name=f"page{i}") for i in range(2)]
+        for page in pages:
+            nc.vector.memset(page[:], 0.0)
+        nc.vector.memset(w4_planes[:].rearrange("p a n -> p (a n)").bitcast(I32), 0)
+
+        def load_w1(b, a):
+            raw = ring.tile([P, PACK, PASS], F32, name=f"w1_raw{b}{a}", tag="w1_raw", bufs=3)
+            rows = w1[a * PASS : (a + 1) * PASS, b * PASS : (b + 1) * PASS]
+            nc.sync.dma_start(raw[:], rows.rearrange("(p j) c -> p j c", j=PACK))
+            return raw
+
+        def load_table(a):
+            words = ring.tile([P, T], U32, name=f"tab{a}", tag=f"big{a}", align_bytes=64)
+            nc.sync.dma_start(words[:].bitcast(I32), tab_words[a].rearrange("p t i -> p (t i)").bitcast(I32))
+            return words
+
+        w1_raw = {(0, a): load_w1(0, a) for a in range(K_PASSES - 1)}
+        nc.sync.dma_start(offs_t[:], offs)
+        for q in range(4):
+            nc.sync.dma_start(
+                tab_planes[32 * q : 32 * q + 4 * K_PASSES, :].bitcast(I32),
+                tab_scales[:, 4 * q : 4 * q + 4, :].bitcast(I32),
+            )
+        w1_raw[0, K_PASSES - 1] = load_w1(0, K_PASSES - 1)
+        tab = [load_table(0)]
+        nc.sync.dma_start(b1_t[:], b1.rearrange("(b p i) -> p b i", b=H_PASSES, i=PACK))
+        nc.sync.dma_start(gain_t[:], gain.rearrange("(b p i) -> p b i", b=H_PASSES, i=PACK))
+        tab.append(load_table(1))
+        nc.sync.dma_start(offs2_t[:], offs2)
+        tab.append(load_table(2))
+        wgs_t = [keep.tile([P, BANK], F32, name=f"wgs{c}") for c in range(S // BANK)]
+        for c in range(S // BANK):
+            nc.sync.dma_start(wgs_t[c][:], wgs[:, c * BANK : (c + 1) * BANK])
+
+        w1_codes, w1_planes = {}, {}
+
+        def quantise_w1(b, a):
+            if (b, a) == (H_PASSES - 1, K_PASSES - 1):
+                grouped = ring.tile([P, PACK * PASS], BF16, name=f"w1_bf{b}{a}", tag="hold", align_bytes=64)
+            else:
+                grouped = ring.tile([P, PACK * PASS], BF16, name=f"w1_bf{b}{a}", tag="w1_bf", bufs=2, align_bytes=64)
+            nc.scalar.copy(
+                grouped[:].rearrange("p (t m j) -> p m t j", t=PACK, j=PACK),
+                w1_raw[b, a][:].rearrange("p j (m t) -> p m t j", t=PACK),
+            )
+            w1_codes[b, a] = keep.tile([P, PASS], U32, name=f"w1_codes{b}{a}", align_bytes=64)
+            w1_planes[b, a] = keep.tile([P, PASS], U8, name=f"w1_plane{b}{a}", align_bytes=64)
+            nc.vector.quantize_mx(w1_codes[b, a][:].bitcast(FP8X4), w1_planes[b, a][:], grouped[:])
+
+        for a in range(K_PASSES):
+            quantise_w1(0, a)
+
+        v_planes = keep.tile([P, S], U8, name="v_planes", align_bytes=64)
+        nc.vector.tensor_copy(v_planes[:], tab_planes[:].indirect(offs_t[:]))
+        v_codes = [keep.tile([P, S], U32, name=f"v_codes{a}", align_bytes=64) for a in range(K_PASSES)]
+        for a in range(K_PASSES - 1):
+            nc.vector.tensor_copy(v_codes[a][:], tab[a][:].indirect(offs_t[:]))
+        for c in range(S // BANK):
+            nc.vector.tensor_copy(
+                v_codes[-1][:, c * BANK : (c + 1) * BANK],
+                tab[-1][:].indirect(entries(offs_t, c * BANK, (c + 1) * BANK)),
+            )
+
+        tanh_t, weight_t = {}, {}
+
+        def respond(b, i, c):
+            if c == 0:
+                tanh_t[b, i] = ring.tile([P, S], F32, name=f"tanh{b}{i}", tag="tanh", bufs=4)
+                weight_t[b, i] = ring.tile([P, S], F32, name=f"weight{b}{i}", tag="weight", bufs=4)
+            cols = slice(c * BANK, (c + 1) * BANK)
+            rows = slice(i * P, (i + 1) * P)
+            nc.scalar.activation(weight_t[b, i][:, cols], wgs_t[c][:], ACT.Copy, scale=gain_t[:, b, i : i + 1])
+            acc = psum.tile([P, BANK], F32, name=f"resp{b}{i}{c}", tag="acc", bufs=4)
+            for a in range(K_PASSES):
+                nc.tensor.matmul_mx(
+                    acc[:],
+                    lhsT=w1_codes[b, a][:, rows].bitcast(FP8X4),
+                    lhsT_scale=w1_planes[b, a][:, rows],
+                    rhs=v_codes[a][:, cols].bitcast(FP8X4),
+                    rhs_scale=v_planes[4 * a : P, cols],
+                    start=(a == 0),
+                    stop=(a == K_PASSES - 1),
+                )
+            nc.scalar.activation(tanh_t[b, i][:, cols], acc[:], ACT.Tanh, bias=b1_t[:, b, i : i + 1])
+
+        def put(b, i, lo, hi):
+            nc.vector.tensor_tensor(
+                pages[i % 2][:].indirect(entries(offs2_t, lo, hi)), tanh_t[b, i][:, lo:hi], weight_t[b, i][:, lo:hi], MULT
+            )
+
+        for c in range(S // BANK):
+            for i in range(2):
+                respond(0, i, c)
+            for i in range(2):
+                put(0, i, c * BANK, (c + 1) * BANK)
+        for i in range(2, PACK):
+            for c in range(S // BANK):
+                respond(0, i, c)
+
+        def load_room(b):
+            room_b = ring.tile([P, PACK, M], F32, name=f"room{b}", tag=f"big{b}", align_bytes=64)
+            nc.sync.dma_start(room_b[:], room[b * PASS : (b + 1) * PASS, :].rearrange("(p i) m -> p i m", i=PACK))
+            return room_b
+
+        wgt_t = keep.tile([P, M], F32, name="wgt_t")
+        nc.sync.dma_start(offs3_t[:], offs3)
+        nc.sync.dma_start(wgt_t[:], wgt)
+        room_t = [load_room(0)]
+        for a in range(K_PASSES):
+            w1_raw[1, a] = load_w1(1, a)
+        room_t.append(load_room(1))
+        w4_codes = keep.tile([P, H_PASSES, 2 * N], U8, name="w4_codes", align_bytes=64)
+        nc.sync.dma_start(w4_codes[:].bitcast(I32), w4_words.rearrange("a p c -> p a c").bitcast(I32))
+        for q in range(4):
+            nc.sync.dma_start(
+                w4_planes[32 * q : 32 * q + 4, :, :].bitcast(I32),
+                w4_scales[:, 4 * q : 4 * q + 4, :].rearrange("a r n -> r a n").bitcast(I32),
+            )
+        b2_t = keep.tile([P, N // P], F32, name="b2_t")
+        with nc.allow_non_contiguous_dma(reason="one bias value to a partition"):
+            nc.sync.dma_start(b2_t[:], b2.rearrange("(c p) -> p c", p=P))
+
+        z_codes = [keep.tile([P, M], U32, name=f"z_codes{b}", align_bytes=64) for b in range(H_PASSES)]
+        z_planes = [keep.tile([P, M], U8, name=f"z_plane{b}", align_bytes=64) for b in range(H_PASSES)]
+
+        def pick(i, lo, hi, picked):
+            nc.vector.tensor_tensor(picked, pages[i % 2][:].indirect(entries(offs3_t, lo, hi)), wgt_t[:, lo:hi], MULT)
+
+        def join(b, u, lo, picked, grouped):
+            total = psum.tile([P, 2, 2, P], F32, name=f"total{b}{u}_{lo}", tag="total", bufs=2)
+            places = [(mb, e, slice(lo + mb * P, lo + (mb + 1) * P)) for e in range(2) for mb in range(2)]
+            for n, (mb, e, cols) in enumerate(places):
+                nc.tensor.matmul(
+                    total[:, mb, e, :], room_t[b][:, 2 * u + e, cols], ident[:], start=(n == 0), stop=False, is_transpose=True
+                )
+            for n, (mb, e, cols) in enumerate(places):
+                nc.tensor.matmul(
+                    total[:, mb, e, :], picked[e][:, cols], ident[:], start=False, stop=(n == 3), is_transpose=True
+                )
+            if (b, lo) == (H_PASSES - 1, M - 2 * P):
+                turned = ring.tile([P, PASS], BF16, name=f"turned{b}{u}_{lo}", tag="big2", align_bytes=64)
+            else:
+                turned = ring.tile([P, PASS], BF16, name=f"turned{b}{u}_{lo}", tag="turned", bufs=3)
+            nc.scalar.copy(
+                turned[:].rearrange("m (mb p e) -> m mb p e", mb=2, e=2),
+                total[:].rearrange("m mb e p -> m mb p e"),
+            )
+            back = psum.tile([P, 2 * P], F32, name=f"back{b}{u}_{lo}", tag="back", bufs=2)
+            for mb in range(2):
+                nc.tensor.transpose(back[:, mb * P : (mb + 1) * P], turned[:].bitcast(F32)[:, mb * P : (mb + 1) * P], ident[:])
+            nc.scalar.copy(grouped.bitcast(F32).rearrange("p (m u) -> p m u", u=2)[:, :, u], back[:])
+
+        def quantise_z(b, lo, hi, grouped):
+            nc.vector.quantize_mx(z_codes[b][:, lo:hi].bitcast(FP8X4), z_planes[b][:, lo:hi], grouped)
+
+        def features(b, banks, lo, hi):
+            for acc, chunks in banks:
+                steps = [(n, c, m0) for n, c in enumerate(chunks) for m0 in range(lo, hi, P)]
+                for step in steps:
+                    n, c, m0 = step
+                    nc.tensor.matmul_mx(
+                        acc[:, n, m0 - lo : m0 - lo + P],
+                        lhsT=w4_codes[:, b, 2 * c * P : 2 * (c + 1) * P].bitcast(FP4X4),
+                        lhsT_scale=w4_planes[:, b, c * P : (c + 1) * P],
+                        rhs=z_codes[b][:, m0 : m0 + P].bitcast(FP8X4),
+                        rhs_scale=z_planes[b][:, m0 : m0 + P],
+                        start=(b == 0 and step == steps[0]),
+                        stop=(b == H_PASSES - 1 and step == steps[-1]),
+                    )
+
+        def finish(banks, lo, hi):
+            result = keep.tile([P, N // P, hi - lo], F32, name=f"result{lo}")
+            for acc, chunks in banks:
+                for n, c in enumerate(chunks):
+                    if hi == M:
+                        nc.vector.tensor_scalar(result[:, c, :], acc[:, n, :], b2_t[:, c : c + 1], None, ADD)
+                    else:
+                        nc.scalar.activation(result[:, c, :], acc[:, n, :], ACT.Identity, bias=b2_t[:, c : c + 1])
+            nc.sync.dma_start(out[:, lo:hi].rearrange("(c p) m -> p c m", p=P), result[:])
+
+        piece = 2 * P
+        grouped0 = ring.tile([P, PACK * M], BF16, name="grouped0", tag="after_z0", align_bytes=64)
+        grouped1 = [keep.tile([P, PACK * piece], BF16, name=f"grouped1_{lo}", align_bytes=64) for lo in range(0, M, piece)]
+        grouped = {}
+        for lo in range(0, M, piece):
+            grouped[0, lo] = grouped0[:, PACK * lo : PACK * (lo + piece)]
+            grouped[1, lo] = grouped1[lo // piece][:]
+
+        def pick_pair(b, u, tag):
+            both = ring.tile([P, 2, M], F32, name=f"picked{b}{u}", tag=tag, align_bytes=64)
+            pick(0, 0, M, both[:, 0, :])
+            if (b, u) == (H_PASSES - 1, 1):
+                for lo in range(0, M, BANK):
+                    pick(1, lo, lo + BANK, both[:, 1, lo : lo + BANK])
+            else:
+                pick(1, 0, M, both[:, 1, :])
+            return both
+
+        def join_pair(b, u, both):
+            for lo in range(0, M, piece):
+                join(b, u, lo, [both[:, 0, :], both[:, 1, :]], grouped[b, lo])
+
+        picked = pick_pair(0, 0, "big2")
+        put(0, 2, 0, S)
+        put(0, 3, 0, S)
+        join_pair(0, 0, picked)
+        for a in range(K_PASSES):
+            quantise_w1(1, a)
+        for i in range(2):
+            for c in range(S // BANK):
+                respond(1, i, c)
+        picked = pick_pair(0, 1, "hold")
+        put(1, 0, 0, S)
+        put(1, 1, 0, S)
+        for i in range(2, PACK):
+            for c in range(S // BANK):
+                respond(1, i, c)
+        join_pair(0, 1, picked)
+        quantise_z(0, 0, M, grouped0[:])
+        picked = pick_pair(1, 0, "after_z0")
+        put(1, 2, 0, S)
+        put(1, 3, 0, S)
+        join_pair(1, 0, picked)
+
+        spans, banks, taken = [], {}, 0
+        bank_tags = [("acc", 4)] * 4 + [("total", 2)] * 2 + [("back", 2)] * 2
+        for width in LAST_PIECES:
+            lo = spans[-1][1] if spans else 0
+            spans.append((lo, lo + width))
+            per_bank = BANK // width
+            banks[lo] = []
+            for c in range(0, N // P, per_bank):
+                chunks = range(c, min(c + per_bank, N // P))
+                tag, bufs = bank_tags[taken]
+                taken = taken + 1
+                acc = psum.tile([P, len(chunks), width], F32, name=f"out{lo}_{c}", tag=tag, bufs=bufs)
+                banks[lo].append((acc, chunks))
+            features(0, banks[lo], lo, lo + width)
+
+        picked = pick_pair(1, 1, "big2")
+
+        def words_of(lo, hi):
+            base = lo // piece * piece
+            return grouped[1, base][:, PACK * (lo - base) : PACK * (hi - base)]
+
+        def add_room(lo, hi):
+            nc.vector.tensor_tensor(
+                words_of(lo, hi).rearrange("p (m u e) -> p m u e", u=2, e=2)[:, :, 1, :],
+                picked[:, :, lo:hi].rearrange("p e m -> p m e"),
+                room_t[1][:, 2:4, lo:hi].rearrange("p e m -> p m e"),
+                ADD,
+            )
+
+        def conclude(lo, hi):
+            quantise_z(1, lo, hi, words_of(lo, hi))
+            features(1, banks[lo], lo, hi)
+            finish(banks[lo], lo, hi)
+
+        add_room(*spans[0])
+        for before, span in zip(spans, spans[1:]):
+            add_room(*span)
+            conclude(*before)
+        conclude(*spans[-1])

@@ -93,7 +93,7 @@ def tile_list_organ_pipe_voicing_kernel(
         w1_codes, w1_planes = {}, {}
 
         def quantise_w1(b, a):
-            if (b, a) == (H_PASSES - 1, K_PASSES - 1):
+            if (b, a) == (H_PASSES - 1, 0):
                 grouped = ring.tile([P, PACK * PASS], BF16, name=f"w1_bf{b}{a}", tag="hold", align_bytes=64)
             else:
                 grouped = ring.tile([P, PACK * PASS], BF16, name=f"w1_bf{b}{a}", tag="w1_bf", bufs=2, align_bytes=64)
@@ -101,7 +101,10 @@ def tile_list_organ_pipe_voicing_kernel(
                 grouped[:].rearrange("p (t m j) -> p m t j", t=PACK, j=PACK),
                 w1_raw[b, a][:].rearrange("p j (m t) -> p m t j", t=PACK),
             )
-            w1_codes[b, a] = keep.tile([P, PASS], U32, name=f"w1_codes{b}{a}", align_bytes=64)
+            if (b, a) == (H_PASSES - 1, 0):
+                w1_codes[b, a] = ring.tile([P, PASS], U32, name=f"w1_codes{b}{a}", tag="big2", align_bytes=64)
+            else:
+                w1_codes[b, a] = keep.tile([P, PASS], U32, name=f"w1_codes{b}{a}", align_bytes=64)
             w1_planes[b, a] = keep.tile([P, PASS], U8, name=f"w1_plane{b}{a}", align_bytes=64)
             nc.vector.quantize_mx(w1_codes[b, a][:].bitcast(FP8X4), w1_planes[b, a][:], grouped[:])
 
@@ -163,10 +166,9 @@ def tile_list_organ_pipe_voicing_kernel(
         wgt_t = keep.tile([P, M], F32, name="wgt_t")
         nc.sync.dma_start(offs3_t[:], offs3)
         nc.sync.dma_start(wgt_t[:], wgt)
-        room_t = [load_room(0)]
         for a in range(K_PASSES):
             w1_raw[1, a] = load_w1(1, a)
-        room_t.append(load_room(1))
+        room_t = [load_room(b) for b in range(H_PASSES)]
         w4_codes = keep.tile([P, H_PASSES, 2 * N], U8, name="w4_codes", align_bytes=64)
         nc.sync.dma_start(w4_codes[:].bitcast(I32), w4_words.rearrange("a p c -> p a c").bitcast(I32))
         for q in range(4):
@@ -303,9 +305,9 @@ def tile_list_organ_pipe_voicing_kernel(
 
         def add_room(lo, hi):
             nc.vector.tensor_tensor(
-                words_of(lo, hi).rearrange("p (m u e) -> p m u e", u=2, e=2)[:, :, 1, :],
-                picked[:, :, lo:hi].rearrange("p e m -> p m e"),
-                room_t[1][:, 2:4, lo:hi].rearrange("p e m -> p m e"),
+                words_of(lo, hi).rearrange("p (m k u e) -> p u m e k", k=2, u=2, e=2)[:, 1, :, :, :],
+                picked[:, :, lo:hi].rearrange("p e (m k) -> p m e k", k=2),
+                room_t[1][:, 2:4, lo:hi].rearrange("p e (m k) -> p m e k", k=2),
                 ADD,
             )
 

@@ -45,12 +45,14 @@ def tile_list_organ_pipe_voicing_kernel(
         offs2_t = keep.tile([P, S // STRIPE], U16, name="offs2_t")
         offs3_t = keep.tile([P, M // STRIPE], U16, name="offs3_t")
 
-        tab_planes = keep.tile([P, T], U8, name="tab_planes", align_bytes=64)
+        tab_planes = ring.tile([P, T], U8, name="tab_planes", tag="scales_first", align_bytes=64)
         w4_planes = keep.tile([P, H_PASSES, N], U8, name="w4_planes", align_bytes=64)
         nc.gpsimd.memset(tab_planes[:].bitcast(I32), 0)
-        warm = keep.tile([P, 2], F32, name="warm")
-        nc.vector.memset(warm[:, 0:1], 0.0)
-        nc.scalar.activation(warm[:, 1:2], warm[:, 0:1], ACT.Tanh)
+        for q in range(4):
+            nc.gpsimd.dma_start(
+                tab_planes[32 * q : 32 * q + 4 * K_PASSES, :].bitcast(I32),
+                tab_scales[:, 4 * q : 4 * q + 4, :].bitcast(I32),
+            )
         b1_t = keep.tile([P, H_PASSES, PACK], F32, name="b1_t")
         gain_t = keep.tile([P, H_PASSES, PACK], F32, name="gain_t")
         ident = keep.tile([P, P], F32, name="ident")
@@ -74,11 +76,6 @@ def tile_list_organ_pipe_voicing_kernel(
 
         w1_raw = {(0, a): load_w1(0, a) for a in range(K_PASSES - 1)}
         nc.sync.dma_start(offs_t[:], offs)
-        for q in range(4):
-            nc.sync.dma_start(
-                tab_planes[32 * q : 32 * q + 4 * K_PASSES, :].bitcast(I32),
-                tab_scales[:, 4 * q : 4 * q + 4, :].bitcast(I32),
-            )
         w1_raw[0, K_PASSES - 1] = load_w1(0, K_PASSES - 1)
         tab = [load_table(0)]
         nc.sync.dma_start(b1_t[:], b1.rearrange("(b p i) -> p b i", b=H_PASSES, i=PACK))
@@ -92,8 +89,8 @@ def tile_list_organ_pipe_voicing_kernel(
 
         w1_codes, w1_planes = {}, {}
 
-        def quantise_w1(b, a):
-            if (b, a) == (H_PASSES - 1, 0):
+        def quantise_w1(b, a, codes):
+            if (b, a) == (H_PASSES - 1, K_PASSES - 1):
                 grouped = ring.tile([P, PACK * PASS], BF16, name=f"w1_bf{b}{a}", tag="hold", align_bytes=64)
             else:
                 grouped = ring.tile([P, PACK * PASS], BF16, name=f"w1_bf{b}{a}", tag="w1_bf", bufs=2, align_bytes=64)
@@ -101,19 +98,18 @@ def tile_list_organ_pipe_voicing_kernel(
                 grouped[:].rearrange("p (t m j) -> p m t j", t=PACK, j=PACK),
                 w1_raw[b, a][:].rearrange("p j (m t) -> p m t j", t=PACK),
             )
-            if (b, a) == (H_PASSES - 1, 0):
-                w1_codes[b, a] = ring.tile([P, PASS], U32, name=f"w1_codes{b}{a}", tag="big2", align_bytes=64)
-            else:
-                w1_codes[b, a] = keep.tile([P, PASS], U32, name=f"w1_codes{b}{a}", align_bytes=64)
+            w1_codes[b, a] = codes[:, a, :]
             w1_planes[b, a] = keep.tile([P, PASS], U8, name=f"w1_plane{b}{a}", align_bytes=64)
-            nc.vector.quantize_mx(w1_codes[b, a][:].bitcast(FP8X4), w1_planes[b, a][:], grouped[:])
+            nc.vector.quantize_mx(w1_codes[b, a].bitcast(FP8X4), w1_planes[b, a][:], grouped[:])
 
+        codes0 = keep.tile([P, K_PASSES, PASS], U32, name="codes0", align_bytes=64)
         for a in range(K_PASSES):
-            quantise_w1(0, a)
+            quantise_w1(0, a, codes0)
 
         v_planes = keep.tile([P, S], U8, name="v_planes", align_bytes=64)
         nc.vector.tensor_copy(v_planes[:], tab_planes[:].indirect(offs_t[:]))
-        v_codes = [keep.tile([P, S], U32, name=f"v_codes{a}", align_bytes=64) for a in range(K_PASSES)]
+        v_codes = [ring.tile([P, S], U32, name="v_codes0", tag="scales_first", align_bytes=64)]
+        v_codes.extend(keep.tile([P, S], U32, name=f"v_codes{a}", align_bytes=64) for a in range(1, K_PASSES))
         for a in range(K_PASSES - 1):
             nc.vector.tensor_copy(v_codes[a][:], tab[a][:].indirect(offs_t[:]))
         for c in range(S // BANK):
@@ -124,13 +120,10 @@ def tile_list_organ_pipe_voicing_kernel(
 
         tanh_t, weight_t = {}, {}
 
-        def respond(b, i, c):
-            if c == 0:
-                tanh_t[b, i] = ring.tile([P, S], F32, name=f"tanh{b}{i}", tag="tanh", bufs=4)
-                weight_t[b, i] = ring.tile([P, S], F32, name=f"weight{b}{i}", tag="weight", bufs=4)
+        def respond(b, i, c, tanh_out, weight_out):
             cols = slice(c * BANK, (c + 1) * BANK)
             rows = slice(i * P, (i + 1) * P)
-            nc.scalar.activation(weight_t[b, i][:, cols], wgs_t[c][:], ACT.Copy, scale=gain_t[:, b, i : i + 1])
+            nc.scalar.activation(weight_out, wgs_t[c][:], ACT.Copy, scale=gain_t[:, b, i : i + 1])
             acc = psum.tile([P, BANK], F32, name=f"resp{b}{i}{c}", tag="acc", bufs=4)
             for a in range(K_PASSES):
                 nc.tensor.matmul_mx(
@@ -142,21 +135,36 @@ def tile_list_organ_pipe_voicing_kernel(
                     start=(a == 0),
                     stop=(a == K_PASSES - 1),
                 )
-            nc.scalar.activation(tanh_t[b, i][:, cols], acc[:], ACT.Tanh, bias=b1_t[:, b, i : i + 1])
+            nc.scalar.activation(tanh_out, acc[:], ACT.Tanh, bias=b1_t[:, b, i : i + 1])
 
-        def put(b, i, lo, hi):
-            nc.vector.tensor_tensor(
-                pages[i % 2][:].indirect(entries(offs2_t, lo, hi)), tanh_t[b, i][:, lo:hi], weight_t[b, i][:, lo:hi], MULT
-            )
+        def put(i, lo, hi, values, weights):
+            nc.vector.tensor_tensor(pages[i % 2][:].indirect(entries(offs2_t, lo, hi)), values, weights, MULT)
 
         for c in range(S // BANK):
+            halves = []
             for i in range(2):
-                respond(0, i, c)
+                tag = "weights" if (i, c) == (0, 0) else f"tanh_half{i}{c}"
+                values = ring.tile([P, BANK], F32, name=f"tanh_half{i}{c}", tag=tag)
+                weights = ring.tile([P, BANK], F32, name=f"weight_half{i}{c}", tag="w1_bf", bufs=2, align_bytes=64)
+                respond(0, i, c, values[:], weights[:])
+                halves.append((values[:], weights[:]))
             for i in range(2):
-                put(0, i, c * BANK, (c + 1) * BANK)
-        for i in range(2, PACK):
+                put(i, c * BANK, (c + 1) * BANK, *halves[i])
+
+        later_weights = ring.tile([P, H_PASSES * PACK - 2, S], F32, name="later_weights", tag="weights")
+
+        def respond_whole(b, i):
+            tanh_t[b, i] = ring.tile([P, S], F32, name=f"tanh{b}{i}", tag="tanh", bufs=4)
+            weight_t[b, i] = later_weights[:, b * PACK + i - 2, :]
             for c in range(S // BANK):
-                respond(0, i, c)
+                cols = slice(c * BANK, (c + 1) * BANK)
+                respond(b, i, c, tanh_t[b, i][:, cols], weight_t[b, i][:, cols])
+
+        def put_whole(b, i):
+            put(i, 0, S, tanh_t[b, i][:], weight_t[b, i])
+
+        for i in range(2, PACK):
+            respond_whole(0, i)
 
         def load_room(b):
             room_b = ring.tile([P, PACK, M], F32, name=f"room{b}", tag=f"big{b}", align_bytes=64)
@@ -261,25 +269,24 @@ def tile_list_organ_pipe_voicing_kernel(
                 join(b, u, lo, [both[:, 0, :], both[:, 1, :]], grouped[b, lo])
 
         picked = pick_pair(0, 0, "big2")
-        put(0, 2, 0, S)
-        put(0, 3, 0, S)
+        put_whole(0, 2)
+        put_whole(0, 3)
         join_pair(0, 0, picked)
+        codes1 = ring.tile([P, K_PASSES, PASS], U32, name="codes1", tag="big2", align_bytes=64)
         for a in range(K_PASSES):
-            quantise_w1(1, a)
+            quantise_w1(1, a, codes1)
         for i in range(2):
-            for c in range(S // BANK):
-                respond(1, i, c)
+            respond_whole(1, i)
         picked = pick_pair(0, 1, "hold")
-        put(1, 0, 0, S)
-        put(1, 1, 0, S)
+        put_whole(1, 0)
+        put_whole(1, 1)
         for i in range(2, PACK):
-            for c in range(S // BANK):
-                respond(1, i, c)
+            respond_whole(1, i)
         join_pair(0, 1, picked)
         quantise_z(0, 0, M, grouped0[:])
         picked = pick_pair(1, 0, "after_z0")
-        put(1, 2, 0, S)
-        put(1, 3, 0, S)
+        put_whole(1, 2)
+        put_whole(1, 3)
         join_pair(1, 0, picked)
 
         spans, banks, taken = [], {}, 0

@@ -23,9 +23,13 @@ PACK = 4
 PASS = P * PACK
 K_PASSES = K // PASS
 H_PASSES = H // PASS
+QUADRANTS = 4
 BANK = 512
 STRIPE = 16
-LAST_PIECES = (256, 256, 256, 128, 128)
+PAIR = 2
+JOIN = 2 * P
+LAST_WIDTHS = (256, 256, 256, 128, 128)
+MX_ALIGN = 64
 
 
 def tile_list_organ_pipe_voicing_kernel(
@@ -45,37 +49,39 @@ def tile_list_organ_pipe_voicing_kernel(
         offs2_t = keep.tile([P, S // STRIPE], U16, name="offs2_t")
         offs3_t = keep.tile([P, M // STRIPE], U16, name="offs3_t")
 
-        tab_planes = ring.tile([P, T], U8, name="tab_planes", tag="scales_first", align_bytes=64)
-        w4_planes = keep.tile([P, H_PASSES, N], U8, name="w4_planes", align_bytes=64)
+        tab_planes = keep.tile([P, T], U8, name="tab_planes", align_bytes=MX_ALIGN)
+        w4_planes = keep.tile([P, H_PASSES, N], U8, name="w4_planes", align_bytes=MX_ALIGN)
         nc.gpsimd.memset(tab_planes[:].bitcast(I32), 0)
-        for q in range(4):
-            nc.gpsimd.dma_start(
-                tab_planes[32 * q : 32 * q + 4 * K_PASSES, :].bitcast(I32),
-                tab_scales[:, 4 * q : 4 * q + 4, :].bitcast(I32),
-            )
         b1_t = keep.tile([P, H_PASSES, PACK], F32, name="b1_t")
         gain_t = keep.tile([P, H_PASSES, PACK], F32, name="gain_t")
         ident = keep.tile([P, P], F32, name="ident")
         make_identity(nc, ident[:])
 
-        pages = [keep.tile([P, T2], F32, name=f"page{i}") for i in range(2)]
+        pages = [keep.tile([P, T2], F32, name=f"page{e}") for e in range(PAIR)]
         for page in pages:
             nc.vector.memset(page[:], 0.0)
         nc.vector.memset(w4_planes[:].rearrange("p a n -> p (a n)").bitcast(I32), 0)
 
         def load_w1(b, a):
-            raw = ring.tile([P, PACK, PASS], F32, name=f"w1_raw{b}{a}", tag="w1_raw", bufs=3)
+            raw = ring.tile([P, PACK, PASS], F32, name=f"w1_raw{b}{a}", tag="w1_raw", bufs=K_PASSES)
             rows = w1[a * PASS : (a + 1) * PASS, b * PASS : (b + 1) * PASS]
             nc.sync.dma_start(raw[:], rows.rearrange("(p j) c -> p j c", j=PACK))
             return raw
 
+        table_tags = ("table_or_room0", "table_or_room1", "after_last_reader")
+
         def load_table(a):
-            words = ring.tile([P, T], U32, name=f"tab{a}", tag=f"big{a}", align_bytes=64)
+            words = ring.tile([P, T], U32, name=f"tab{a}", tag=table_tags[a], align_bytes=MX_ALIGN)
             nc.sync.dma_start(words[:].bitcast(I32), tab_words[a].rearrange("p t i -> p (t i)").bitcast(I32))
             return words
 
         w1_raw = {(0, a): load_w1(0, a) for a in range(K_PASSES - 1)}
         nc.sync.dma_start(offs_t[:], offs)
+        for q in range(QUADRANTS):
+            nc.sync.dma_start(
+                tab_planes[32 * q : 32 * q + 4 * K_PASSES, :].bitcast(I32),
+                tab_scales[:, 4 * q : 4 * q + 4, :].bitcast(I32),
+            )
         w1_raw[0, K_PASSES - 1] = load_w1(0, K_PASSES - 1)
         tab = [load_table(0)]
         nc.sync.dma_start(b1_t[:], b1.rearrange("(b p i) -> p b i", b=H_PASSES, i=PACK))
@@ -89,27 +95,28 @@ def tile_list_organ_pipe_voicing_kernel(
 
         w1_codes, w1_planes = {}, {}
 
-        def quantise_w1(b, a, codes):
-            if (b, a) == (H_PASSES - 1, K_PASSES - 1):
-                grouped = ring.tile([P, PACK * PASS], BF16, name=f"w1_bf{b}{a}", tag="hold", align_bytes=64)
-            else:
-                grouped = ring.tile([P, PACK * PASS], BF16, name=f"w1_bf{b}{a}", tag="w1_bf", bufs=2, align_bytes=64)
-            nc.scalar.copy(
-                grouped[:].rearrange("p (t m j) -> p m t j", t=PACK, j=PACK),
-                w1_raw[b, a][:].rearrange("p j (m t) -> p m t j", t=PACK),
-            )
-            w1_codes[b, a] = codes[:, a, :]
-            w1_planes[b, a] = keep.tile([P, PASS], U8, name=f"w1_plane{b}{a}", align_bytes=64)
-            nc.vector.quantize_mx(w1_codes[b, a].bitcast(FP8X4), w1_planes[b, a][:], grouped[:])
+        def quantise_w1(b, codes):
+            for a in range(K_PASSES):
+                if (b, a) == (H_PASSES - 1, K_PASSES - 1):
+                    rounded = ring.tile([P, PACK * PASS], BF16, name="w1_bf_last", tag="after_w1", align_bytes=MX_ALIGN)
+                else:
+                    rounded = ring.tile(
+                        [P, PACK * PASS], BF16, name=f"w1_bf{b}{a}", tag="after_first_puts", bufs=PAIR, align_bytes=MX_ALIGN
+                    )
+                nc.scalar.copy(
+                    rounded[:].rearrange("p (i m j) -> p m i j", i=PACK, j=PACK),
+                    w1_raw[b, a][:].rearrange("p j (m i) -> p m i j", i=PACK),
+                )
+                w1_codes[b, a] = codes[:, a, :]
+                w1_planes[b, a] = keep.tile([P, PASS], U8, name=f"w1_plane{b}{a}", align_bytes=MX_ALIGN)
+                nc.vector.quantize_mx(w1_codes[b, a].bitcast(FP8X4), w1_planes[b, a][:], rounded[:])
 
-        codes0 = keep.tile([P, K_PASSES, PASS], U32, name="codes0", align_bytes=64)
-        for a in range(K_PASSES):
-            quantise_w1(0, a, codes0)
+        codes0 = keep.tile([P, K_PASSES, PASS], U32, name="codes0", align_bytes=MX_ALIGN)
+        quantise_w1(0, codes0)
 
-        v_planes = keep.tile([P, S], U8, name="v_planes", align_bytes=64)
+        v_planes = keep.tile([P, S], U8, name="v_planes", align_bytes=MX_ALIGN)
         nc.vector.tensor_copy(v_planes[:], tab_planes[:].indirect(offs_t[:]))
-        v_codes = [ring.tile([P, S], U32, name="v_codes0", tag="scales_first", align_bytes=64)]
-        v_codes.extend(keep.tile([P, S], U32, name=f"v_codes{a}", align_bytes=64) for a in range(1, K_PASSES))
+        v_codes = [keep.tile([P, S], U32, name=f"v_codes{a}", align_bytes=MX_ALIGN) for a in range(K_PASSES)]
         for a in range(K_PASSES - 1):
             nc.vector.tensor_copy(v_codes[a][:], tab[a][:].indirect(offs_t[:]))
         for c in range(S // BANK):
@@ -117,8 +124,6 @@ def tile_list_organ_pipe_voicing_kernel(
                 v_codes[-1][:, c * BANK : (c + 1) * BANK],
                 tab[-1][:].indirect(entries(offs_t, c * BANK, (c + 1) * BANK)),
             )
-
-        tanh_t, weight_t = {}, {}
 
         def respond(b, i, c, tanh_out, weight_out):
             cols = slice(c * BANK, (c + 1) * BANK)
@@ -138,36 +143,40 @@ def tile_list_organ_pipe_voicing_kernel(
             nc.scalar.activation(tanh_out, acc[:], ACT.Tanh, bias=b1_t[:, b, i : i + 1])
 
         def put(i, lo, hi, values, weights):
-            nc.vector.tensor_tensor(pages[i % 2][:].indirect(entries(offs2_t, lo, hi)), values, weights, MULT)
+            nc.vector.tensor_tensor(pages[i % PAIR][:].indirect(entries(offs2_t, lo, hi)), values, weights, MULT)
 
         for c in range(S // BANK):
             halves = []
-            for i in range(2):
-                tag = "weights" if (i, c) == (0, 0) else f"tanh_half{i}{c}"
+            for i in range(PAIR):
+                tag = "after_first_put" if (i, c) == (0, 0) else f"tanh_half{i}{c}"
                 values = ring.tile([P, BANK], F32, name=f"tanh_half{i}{c}", tag=tag)
-                weights = ring.tile([P, BANK], F32, name=f"weight_half{i}{c}", tag="w1_bf", bufs=2, align_bytes=64)
+                weights = ring.tile(
+                    [P, BANK], F32, name=f"weight_half{i}{c}", tag="after_first_puts", bufs=PAIR, align_bytes=MX_ALIGN
+                )
                 respond(0, i, c, values[:], weights[:])
                 halves.append((values[:], weights[:]))
-            for i in range(2):
+            for i in range(PAIR):
                 put(i, c * BANK, (c + 1) * BANK, *halves[i])
 
-        later_weights = ring.tile([P, H_PASSES * PACK - 2, S], F32, name="later_weights", tag="weights")
+        later_weights = ring.tile([P, H_PASSES * PACK - PAIR, S], F32, name="later_weights", tag="after_first_put")
+        tanh_t, weight_t = {}, {}
 
-        def respond_whole(b, i):
-            tanh_t[b, i] = ring.tile([P, S], F32, name=f"tanh{b}{i}", tag="tanh", bufs=4)
-            weight_t[b, i] = later_weights[:, b * PACK + i - 2, :]
-            for c in range(S // BANK):
-                cols = slice(c * BANK, (c + 1) * BANK)
-                respond(b, i, c, tanh_t[b, i][:, cols], weight_t[b, i][:, cols])
+        def respond_pair(b, u):
+            for i in range(PAIR * u, PAIR * (u + 1)):
+                tanh_t[b, i] = ring.tile([P, S], F32, name=f"tanh{b}{i}", tag="tanh", bufs=2 * PAIR)
+                weight_t[b, i] = later_weights[:, b * PACK + i - PAIR, :]
+                for c in range(S // BANK):
+                    cols = slice(c * BANK, (c + 1) * BANK)
+                    respond(b, i, c, tanh_t[b, i][:, cols], weight_t[b, i][:, cols])
 
-        def put_whole(b, i):
-            put(i, 0, S, tanh_t[b, i][:], weight_t[b, i])
+        def put_pair(b, u):
+            for i in range(PAIR * u, PAIR * (u + 1)):
+                put(i, 0, S, tanh_t[b, i][:], weight_t[b, i])
 
-        for i in range(2, PACK):
-            respond_whole(0, i)
+        respond_pair(0, 1)
 
         def load_room(b):
-            room_b = ring.tile([P, PACK, M], F32, name=f"room{b}", tag=f"big{b}", align_bytes=64)
+            room_b = ring.tile([P, PACK, M], F32, name=f"room{b}", tag=table_tags[b], align_bytes=MX_ALIGN)
             nc.sync.dma_start(room_b[:], room[b * PASS : (b + 1) * PASS, :].rearrange("(p i) m -> p i m", i=PACK))
             return room_b
 
@@ -177,9 +186,9 @@ def tile_list_organ_pipe_voicing_kernel(
         for a in range(K_PASSES):
             w1_raw[1, a] = load_w1(1, a)
         room_t = [load_room(b) for b in range(H_PASSES)]
-        w4_codes = keep.tile([P, H_PASSES, 2 * N], U8, name="w4_codes", align_bytes=64)
+        w4_codes = keep.tile([P, H_PASSES, 2 * N], U8, name="w4_codes", align_bytes=MX_ALIGN)
         nc.sync.dma_start(w4_codes[:].bitcast(I32), w4_words.rearrange("a p c -> p a c").bitcast(I32))
-        for q in range(4):
+        for q in range(QUADRANTS):
             nc.sync.dma_start(
                 w4_planes[32 * q : 32 * q + 4, :, :].bitcast(I32),
                 w4_scales[:, 4 * q : 4 * q + 4, :].rearrange("a r n -> r a n").bitcast(I32),
@@ -188,40 +197,89 @@ def tile_list_organ_pipe_voicing_kernel(
         with nc.allow_non_contiguous_dma(reason="one bias value to a partition"):
             nc.sync.dma_start(b2_t[:], b2.rearrange("(c p) -> p c", p=P))
 
-        z_codes = [keep.tile([P, M], U32, name=f"z_codes{b}", align_bytes=64) for b in range(H_PASSES)]
-        z_planes = [keep.tile([P, M], U8, name=f"z_plane{b}", align_bytes=64) for b in range(H_PASSES)]
+        z_codes = [keep.tile([P, M], U32, name=f"z_codes{b}", align_bytes=MX_ALIGN) for b in range(H_PASSES)]
+        z_planes = [keep.tile([P, M], U8, name=f"z_plane{b}", align_bytes=MX_ALIGN) for b in range(H_PASSES)]
 
-        def pick(i, lo, hi, picked):
-            nc.vector.tensor_tensor(picked, pages[i % 2][:].indirect(entries(offs3_t, lo, hi)), wgt_t[:, lo:hi], MULT)
+        z_bf0 = ring.tile([P, PACK * M], BF16, name="z_bf0", tag="after_z0", align_bytes=MX_ALIGN)
+        z_bf1 = [keep.tile([P, PACK * JOIN], BF16, name=f"z_bf1_{lo}", align_bytes=MX_ALIGN) for lo in range(0, M, JOIN)]
 
-        def join(b, u, lo, picked, grouped):
-            total = psum.tile([P, 2, 2, P], F32, name=f"total{b}{u}_{lo}", tag="total", bufs=2)
-            places = [(mb, e, slice(lo + mb * P, lo + (mb + 1) * P)) for e in range(2) for mb in range(2)]
-            for n, (mb, e, cols) in enumerate(places):
-                nc.tensor.matmul(
-                    total[:, mb, e, :], room_t[b][:, 2 * u + e, cols], ident[:], start=(n == 0), stop=False, is_transpose=True
+        def z_bf(b, lo, hi):
+            if b == 0:
+                return z_bf0[:, PACK * lo : PACK * hi]
+            base = lo // JOIN * JOIN
+            return z_bf1[lo // JOIN][:, PACK * (lo - base) : PACK * (hi - base)]
+
+        def pick(e, lo, hi, picked):
+            nc.vector.tensor_tensor(picked[:, e, lo:hi], pages[e][:].indirect(entries(offs3_t, lo, hi)), wgt_t[:, lo:hi], MULT)
+
+        def pick_pair(b, u, tag):
+            picked = ring.tile([P, PAIR, M], F32, name=f"picked{b}{u}", tag=tag, align_bytes=MX_ALIGN)
+            pick(0, 0, M, picked)
+            width = BANK if (b, u) == (H_PASSES - 1, 1) else M
+            for lo in range(0, M, width):
+                pick(1, lo, lo + width, picked)
+            return picked
+
+        def join_pair(b, u, picked):
+            for lo in range(0, M, JOIN):
+                total = psum.tile([P, JOIN // P, PAIR, P], F32, name=f"total{b}{u}_{lo}", tag="total", bufs=2)
+                places = [
+                    (block, e, slice(lo + block * P, lo + (block + 1) * P)) for e in range(PAIR) for block in range(JOIN // P)
+                ]
+                for n, (block, e, cols) in enumerate(places):
+                    nc.tensor.matmul(
+                        total[:, block, e, :],
+                        room_t[b][:, PAIR * u + e, cols],
+                        ident[:],
+                        start=(n == 0),
+                        stop=False,
+                        is_transpose=True,
+                    )
+                for n, (block, e, cols) in enumerate(places):
+                    nc.tensor.matmul(
+                        total[:, block, e, :],
+                        picked[:, e, cols],
+                        ident[:],
+                        start=False,
+                        stop=(n == len(places) - 1),
+                        is_transpose=True,
+                    )
+                if (b, lo) == (H_PASSES - 1, M - JOIN):
+                    turned = ring.tile(
+                        [P, PAIR * JOIN], BF16, name="turned_last", tag="after_last_reader", align_bytes=MX_ALIGN
+                    )
+                else:
+                    turned = ring.tile([P, PAIR * JOIN], BF16, name=f"turned{b}{u}_{lo}", tag="turned", bufs=3)
+                nc.scalar.copy(
+                    turned[:].rearrange("m (block p e) -> m block p e", block=JOIN // P, e=PAIR),
+                    total[:].rearrange("m block e p -> m block p e"),
                 )
-            for n, (mb, e, cols) in enumerate(places):
-                nc.tensor.matmul(
-                    total[:, mb, e, :], picked[e][:, cols], ident[:], start=False, stop=(n == 3), is_transpose=True
-                )
-            if (b, lo) == (H_PASSES - 1, M - 2 * P):
-                turned = ring.tile([P, PASS], BF16, name=f"turned{b}{u}_{lo}", tag="big2", align_bytes=64)
-            else:
-                turned = ring.tile([P, PASS], BF16, name=f"turned{b}{u}_{lo}", tag="turned", bufs=3)
-            nc.scalar.copy(
-                turned[:].rearrange("m (mb p e) -> m mb p e", mb=2, e=2),
-                total[:].rearrange("m mb e p -> m mb p e"),
-            )
-            back = psum.tile([P, 2 * P], F32, name=f"back{b}{u}_{lo}", tag="back", bufs=2)
-            for mb in range(2):
-                nc.tensor.transpose(back[:, mb * P : (mb + 1) * P], turned[:].bitcast(F32)[:, mb * P : (mb + 1) * P], ident[:])
-            nc.scalar.copy(grouped.bitcast(F32).rearrange("p (m u) -> p m u", u=2)[:, :, u], back[:])
+                back = psum.tile([P, JOIN], F32, name=f"back{b}{u}_{lo}", tag="back", bufs=2)
+                for block in range(JOIN // P):
+                    cols = slice(block * P, (block + 1) * P)
+                    nc.tensor.transpose(back[:, cols], turned[:].bitcast(F32)[:, cols], ident[:])
+                words = z_bf(b, lo, lo + JOIN).bitcast(F32).rearrange("p (m u) -> p m u", u=PACK // PAIR)
+                nc.scalar.copy(words[:, :, u], back[:])
 
-        def quantise_z(b, lo, hi, grouped):
-            nc.vector.quantize_mx(z_codes[b][:, lo:hi].bitcast(FP8X4), z_planes[b][:, lo:hi], grouped)
+        def quantise_z(b, lo, hi):
+            nc.vector.quantize_mx(z_codes[b][:, lo:hi].bitcast(FP8X4), z_planes[b][:, lo:hi], z_bf(b, lo, hi))
 
-        def features(b, banks, lo, hi):
+        picked = pick_pair(0, 0, "after_last_reader")
+        put_pair(0, 1)
+        join_pair(0, 0, picked)
+        codes1 = ring.tile([P, K_PASSES, PASS], U32, name="codes1", tag="after_last_reader", align_bytes=MX_ALIGN)
+        quantise_w1(1, codes1)
+        respond_pair(1, 0)
+        picked = pick_pair(0, 1, "after_w1")
+        put_pair(1, 0)
+        respond_pair(1, 1)
+        join_pair(0, 1, picked)
+        quantise_z(0, 0, M)
+        picked = pick_pair(1, 0, "after_z0")
+        put_pair(1, 1)
+        join_pair(1, 0, picked)
+
+        def multiply(b, banks, lo, hi):
             for acc, chunks in banks:
                 steps = [(n, c, m0) for n, c in enumerate(chunks) for m0 in range(lo, hi, P)]
                 for step in steps:
@@ -236,62 +294,9 @@ def tile_list_organ_pipe_voicing_kernel(
                         stop=(b == H_PASSES - 1 and step == steps[-1]),
                     )
 
-        def finish(banks, lo, hi):
-            result = keep.tile([P, N // P, hi - lo], F32, name=f"result{lo}")
-            for acc, chunks in banks:
-                for n, c in enumerate(chunks):
-                    if hi == M:
-                        nc.vector.tensor_scalar(result[:, c, :], acc[:, n, :], b2_t[:, c : c + 1], None, ADD)
-                    else:
-                        nc.scalar.activation(result[:, c, :], acc[:, n, :], ACT.Identity, bias=b2_t[:, c : c + 1])
-            nc.sync.dma_start(out[:, lo:hi].rearrange("(c p) m -> p c m", p=P), result[:])
-
-        piece = 2 * P
-        grouped0 = ring.tile([P, PACK * M], BF16, name="grouped0", tag="after_z0", align_bytes=64)
-        grouped1 = [keep.tile([P, PACK * piece], BF16, name=f"grouped1_{lo}", align_bytes=64) for lo in range(0, M, piece)]
-        grouped = {}
-        for lo in range(0, M, piece):
-            grouped[0, lo] = grouped0[:, PACK * lo : PACK * (lo + piece)]
-            grouped[1, lo] = grouped1[lo // piece][:]
-
-        def pick_pair(b, u, tag):
-            both = ring.tile([P, 2, M], F32, name=f"picked{b}{u}", tag=tag, align_bytes=64)
-            pick(0, 0, M, both[:, 0, :])
-            if (b, u) == (H_PASSES - 1, 1):
-                for lo in range(0, M, BANK):
-                    pick(1, lo, lo + BANK, both[:, 1, lo : lo + BANK])
-            else:
-                pick(1, 0, M, both[:, 1, :])
-            return both
-
-        def join_pair(b, u, both):
-            for lo in range(0, M, piece):
-                join(b, u, lo, [both[:, 0, :], both[:, 1, :]], grouped[b, lo])
-
-        picked = pick_pair(0, 0, "big2")
-        put_whole(0, 2)
-        put_whole(0, 3)
-        join_pair(0, 0, picked)
-        codes1 = ring.tile([P, K_PASSES, PASS], U32, name="codes1", tag="big2", align_bytes=64)
-        for a in range(K_PASSES):
-            quantise_w1(1, a, codes1)
-        for i in range(2):
-            respond_whole(1, i)
-        picked = pick_pair(0, 1, "hold")
-        put_whole(1, 0)
-        put_whole(1, 1)
-        for i in range(2, PACK):
-            respond_whole(1, i)
-        join_pair(0, 1, picked)
-        quantise_z(0, 0, M, grouped0[:])
-        picked = pick_pair(1, 0, "after_z0")
-        put_whole(1, 2)
-        put_whole(1, 3)
-        join_pair(1, 0, picked)
-
         spans, banks, taken = [], {}, 0
         bank_tags = [("acc", 4)] * 4 + [("total", 2)] * 2 + [("back", 2)] * 2
-        for width in LAST_PIECES:
+        for width in LAST_WIDTHS:
             lo = spans[-1][1] if spans else 0
             spans.append((lo, lo + width))
             per_bank = BANK // width
@@ -302,26 +307,29 @@ def tile_list_organ_pipe_voicing_kernel(
                 taken = taken + 1
                 acc = psum.tile([P, len(chunks), width], F32, name=f"out{lo}_{c}", tag=tag, bufs=bufs)
                 banks[lo].append((acc, chunks))
-            features(0, banks[lo], lo, lo + width)
+            multiply(0, banks[lo], lo, lo + width)
 
-        picked = pick_pair(1, 1, "big2")
-
-        def words_of(lo, hi):
-            base = lo // piece * piece
-            return grouped[1, base][:, PACK * (lo - base) : PACK * (hi - base)]
+        picked = pick_pair(1, 1, "after_last_reader")
 
         def add_room(lo, hi):
             nc.vector.tensor_tensor(
-                words_of(lo, hi).rearrange("p (m k u e) -> p u m e k", k=2, u=2, e=2)[:, 1, :, :, :],
+                z_bf(1, lo, hi).rearrange("p (m k u e) -> p u m e k", k=2, u=PACK // PAIR, e=PAIR)[:, 1, :, :, :],
                 picked[:, :, lo:hi].rearrange("p e (m k) -> p m e k", k=2),
-                room_t[1][:, 2:4, lo:hi].rearrange("p e (m k) -> p m e k", k=2),
+                room_t[1][:, PAIR:PACK, lo:hi].rearrange("p e (m k) -> p m e k", k=2),
                 ADD,
             )
 
         def conclude(lo, hi):
-            quantise_z(1, lo, hi, words_of(lo, hi))
-            features(1, banks[lo], lo, hi)
-            finish(banks[lo], lo, hi)
+            quantise_z(1, lo, hi)
+            multiply(1, banks[lo], lo, hi)
+            result = keep.tile([P, N // P, hi - lo], F32, name=f"result{lo}")
+            for acc, chunks in banks[lo]:
+                for n, c in enumerate(chunks):
+                    if hi == M:
+                        nc.vector.tensor_scalar(result[:, c, :], acc[:, n, :], b2_t[:, c : c + 1], None, ADD)
+                    else:
+                        nc.scalar.activation(result[:, c, :], acc[:, n, :], ACT.Identity, bias=b2_t[:, c : c + 1])
+            nc.sync.dma_start(out[:, lo:hi].rearrange("(c p) m -> p c m", p=P), result[:])
 
         add_room(*spans[0])
         for before, span in zip(spans, spans[1:]):

from contextlib import ExitStack

import concourse.mybir as mybir
from concourse.masks import make_identity

K, H, N, T, S, T2, M = 1536, 1024, 384, 4096, 1024, 2048, 1024
FLOPS = 2 * K * H * S + 2 * H * N * M

F32 = mybir.dt.float32
BF16 = mybir.dt.bfloat16
I32 = mybir.dt.int32
U32 = mybir.dt.uint32
U16 = mybir.dt.uint16
U8 = mybir.dt.uint8
FP8X4 = mybir.dt.float8_e4m3fn_x4
FP4X4 = mybir.dt.float4_e2m1fn_x4
MULT = mybir.AluOpType.mult
ADD = mybir.AluOpType.add
ACT = mybir.ActivationFunctionType

P = 128
PACK = 4
PASS = P * PACK
K_PASSES = K // PASS
H_PASSES = H // PASS
QUADRANTS = 4
BANK = 512
STRIPE = 16
PAIR = 2
JOIN = 2 * P
LAST_WIDTHS = (256, 256, 256, 128, 128)
MX_ALIGN = 64


def tile_list_organ_pipe_voicing_kernel(
    tc, tab_words, tab_scales, offs, w1, b1, gain, offs2, wgs, offs3, wgt, room, w4_words, w4_scales, b2, out
):
    nc = tc.nc

    def entries(list_tile, lo, hi):
        return list_tile[:, lo // STRIPE : hi // STRIPE]

    with ExitStack() as ctx:
        keep = ctx.enter_context(tc.tile_pool(name="keep", bufs=1))
        ring = ctx.enter_context(tc.tile_pool(name="ring", bufs=1))
        psum = ctx.enter_context(tc.psum_pool(name="psum", bufs=1))

        offs_t = keep.tile([P, S // STRIPE], U16, name="offs_t")
        offs2_t = keep.tile([P, S // STRIPE], U16, name="offs2_t")
        offs3_t = keep.tile([P, M // STRIPE], U16, name="offs3_t")

        tab_planes = keep.tile([P, T], U8, name="tab_planes", align_bytes=MX_ALIGN)
        w4_planes = keep.tile([P, H_PASSES, N], U8, name="w4_planes", align_bytes=MX_ALIGN)
        nc.gpsimd.memset(tab_planes[:].bitcast(I32), 0)
        b1_t = keep.tile([P, H_PASSES, PACK], F32, name="b1_t")
        gain_t = keep.tile([P, H_PASSES, PACK], F32, name="gain_t")
        ident = keep.tile([P, P], F32, name="ident")
        make_identity(nc, ident[:])

        pages = [keep.tile([P, T2], F32, name=f"page{e}") for e in range(PAIR)]
        for page in pages:
            nc.vector.memset(page[:], 0.0)
        nc.vector.memset(w4_planes[:].rearrange("p a n -> p (a n)").bitcast(I32), 0)

        def load_w1(b, a):
            raw = ring.tile([P, PACK, PASS], F32, name=f"w1_raw{b}{a}", tag="w1_raw", bufs=K_PASSES)
            rows = w1[a * PASS : (a + 1) * PASS, b * PASS : (b + 1) * PASS]
            nc.sync.dma_start(raw[:], rows.rearrange("(p j) c -> p j c", j=PACK))
            return raw

        table_tags = ("table_or_room0", "table_or_room1", "after_last_reader")

        def load_table(a):
            words = ring.tile([P, T], U32, name=f"tab{a}", tag=table_tags[a], align_bytes=MX_ALIGN)
            nc.sync.dma_start(words[:].bitcast(I32), tab_words[a].rearrange("p t i -> p (t i)").bitcast(I32))
            return words

        w1_raw = {(0, a): load_w1(0, a) for a in range(K_PASSES - 1)}
        nc.sync.dma_start(offs_t[:], offs)
        for q in range(QUADRANTS):
            nc.sync.dma_start(
                tab_planes[32 * q : 32 * q + 4 * K_PASSES, :].bitcast(I32),
                tab_scales[:, 4 * q : 4 * q + 4, :].bitcast(I32),
            )
        w1_raw[0, K_PASSES - 1] = load_w1(0, K_PASSES - 1)
        tab = [load_table(0)]
        nc.sync.dma_start(b1_t[:], b1.rearrange("(b p i) -> p b i", b=H_PASSES, i=PACK))
        nc.sync.dma_start(gain_t[:], gain.rearrange("(b p i) -> p b i", b=H_PASSES, i=PACK))
        tab.append(load_table(1))
        nc.sync.dma_start(offs2_t[:], offs2)
        tab.append(load_table(2))
        wgs_t = [keep.tile([P, BANK], F32, name=f"wgs{c}") for c in range(S // BANK)]
        for c in range(S // BANK):
            nc.sync.dma_start(wgs_t[c][:], wgs[:, c * BANK : (c + 1) * BANK])

        w1_codes, w1_planes = {}, {}

        def quantise_w1(b, codes):
            for a in range(K_PASSES):
                if (b, a) == (H_PASSES - 1, K_PASSES - 1):
                    rounded = ring.tile([P, PACK * PASS], BF16, name="w1_bf_last", tag="after_w1", align_bytes=MX_ALIGN)
                else:
                    rounded = ring.tile(
                        [P, PACK * PASS], BF16, name=f"w1_bf{b}{a}", tag="after_first_puts", bufs=PAIR, align_bytes=MX_ALIGN
                    )
                nc.scalar.copy(
                    rounded[:].rearrange("p (i m j) -> p m i j", i=PACK, j=PACK),
                    w1_raw[b, a][:].rearrange("p j (m i) -> p m i j", i=PACK),
                )
                w1_codes[b, a] = codes[:, a, :]
                w1_planes[b, a] = keep.tile([P, PASS], U8, name=f"w1_plane{b}{a}", align_bytes=MX_ALIGN)
                nc.vector.quantize_mx(w1_codes[b, a].bitcast(FP8X4), w1_planes[b, a][:], rounded[:])

        codes0 = keep.tile([P, K_PASSES, PASS], U32, name="codes0", align_bytes=MX_ALIGN)
        quantise_w1(0, codes0)

        v_planes = keep.tile([P, S], U8, name="v_planes", align_bytes=MX_ALIGN)
        nc.vector.tensor_copy(v_planes[:], tab_planes[:].indirect(offs_t[:]))
        v_codes = [keep.tile([P, S], U32, name=f"v_codes{a}", align_bytes=MX_ALIGN) for a in range(K_PASSES)]
        for a in range(K_PASSES - 1):
            nc.vector.tensor_copy(v_codes[a][:], tab[a][:].indirect(offs_t[:]))
        for c in range(S // BANK):
            nc.vector.tensor_copy(
                v_codes[-1][:, c * BANK : (c + 1) * BANK],
                tab[-1][:].indirect(entries(offs_t, c * BANK, (c + 1) * BANK)),
            )

        def respond(b, i, c, tanh_out, weight_out):
            cols = slice(c * BANK, (c + 1) * BANK)
            rows = slice(i * P, (i + 1) * P)
            nc.scalar.activation(weight_out, wgs_t[c][:], ACT.Copy, scale=gain_t[:, b, i : i + 1])
            acc = psum.tile([P, BANK], F32, name=f"resp{b}{i}{c}", tag="acc", bufs=4)
            for a in range(K_PASSES):
                nc.tensor.matmul_mx(
                    acc[:],
                    lhsT=w1_codes[b, a][:, rows].bitcast(FP8X4),
                    lhsT_scale=w1_planes[b, a][:, rows],
                    rhs=v_codes[a][:, cols].bitcast(FP8X4),
                    rhs_scale=v_planes[4 * a : P, cols],
                    start=(a == 0),
                    stop=(a == K_PASSES - 1),
                )
            nc.scalar.activation(tanh_out, acc[:], ACT.Tanh, bias=b1_t[:, b, i : i + 1])

        def put(i, lo, hi, values, weights):
            nc.vector.tensor_tensor(pages[i % PAIR][:].indirect(entries(offs2_t, lo, hi)), values, weights, MULT)

        for c in range(S // BANK):
            halves = []
            for i in range(PAIR):
                tag = "after_first_put" if (i, c) == (0, 0) else f"tanh_half{i}{c}"
                values = ring.tile([P, BANK], F32, name=f"tanh_half{i}{c}", tag=tag)
                weights = ring.tile(
                    [P, BANK], F32, name=f"weight_half{i}{c}", tag="after_first_puts", bufs=PAIR, align_bytes=MX_ALIGN
                )
                respond(0, i, c, values[:], weights[:])
                halves.append((values[:], weights[:]))
            for i in range(PAIR):
                put(i, c * BANK, (c + 1) * BANK, *halves[i])

        later_weights = ring.tile([P, H_PASSES * PACK - PAIR, S], F32, name="later_weights", tag="after_first_put")
        tanh_t, weight_t = {}, {}

        def respond_pair(b, u):
            for i in range(PAIR * u, PAIR * (u + 1)):
                tanh_t[b, i] = ring.tile([P, S], F32, name=f"tanh{b}{i}", tag="tanh", bufs=2 * PAIR)
                weight_t[b, i] = later_weights[:, b * PACK + i - PAIR, :]
                for c in range(S // BANK):
                    cols = slice(c * BANK, (c + 1) * BANK)
                    respond(b, i, c, tanh_t[b, i][:, cols], weight_t[b, i][:, cols])

        def put_pair(b, u):
            for i in range(PAIR * u, PAIR * (u + 1)):
                put(i, 0, S, tanh_t[b, i][:], weight_t[b, i])

        respond_pair(0, 1)

        def load_room(b):
            room_b = ring.tile([P, PACK, M], F32, name=f"room{b}", tag=table_tags[b], align_bytes=MX_ALIGN)
            nc.sync.dma_start(room_b[:], room[b * PASS : (b + 1) * PASS, :].rearrange("(p i) m -> p i m", i=PACK))
            return room_b

        wgt_t = keep.tile([P, M], F32, name="wgt_t")
        nc.sync.dma_start(offs3_t[:], offs3)
        nc.sync.dma_start(wgt_t[:], wgt)
        for a in range(K_PASSES):
            w1_raw[1, a] = load_w1(1, a)
        room_t = [load_room(b) for b in range(H_PASSES)]
        w4_codes = keep.tile([P, H_PASSES, 2 * N], U8, name="w4_codes", align_bytes=MX_ALIGN)
        nc.sync.dma_start(w4_codes[:].bitcast(I32), w4_words.rearrange("a p c -> p a c").bitcast(I32))
        for q in range(QUADRANTS):
            nc.sync.dma_start(
                w4_planes[32 * q : 32 * q + 4, :, :].bitcast(I32),
                w4_scales[:, 4 * q : 4 * q + 4, :].rearrange("a r n -> r a n").bitcast(I32),
            )
        b2_t = keep.tile([P, N // P], F32, name="b2_t")
        with nc.allow_non_contiguous_dma(reason="one bias value to a partition"):
            nc.sync.dma_start(b2_t[:], b2.rearrange("(c p) -> p c", p=P))

        z_codes = [keep.tile([P, M], U32, name=f"z_codes{b}", align_bytes=MX_ALIGN) for b in range(H_PASSES)]
        z_planes = [keep.tile([P, M], U8, name=f"z_plane{b}", align_bytes=MX_ALIGN) for b in range(H_PASSES)]

        z_bf0 = ring.tile([P, PACK * M], BF16, name="z_bf0", tag="after_z0", align_bytes=MX_ALIGN)
        z_bf1 = [keep.tile([P, PACK * JOIN], BF16, name=f"z_bf1_{lo}", align_bytes=MX_ALIGN) for lo in range(0, M, JOIN)]

        def z_bf(b, lo, hi):
            if b == 0:
                return z_bf0[:, PACK * lo : PACK * hi]
            base = lo // JOIN * JOIN
            return z_bf1[lo // JOIN][:, PACK * (lo - base) : PACK * (hi - base)]

        def pick(e, lo, hi, picked):
            nc.vector.tensor_tensor(picked[:, e, lo:hi], pages[e][:].indirect(entries(offs3_t, lo, hi)), wgt_t[:, lo:hi], MULT)

        def pick_pair(b, u, tag):
            picked = ring.tile([P, PAIR, M], F32, name=f"picked{b}{u}", tag=tag, align_bytes=MX_ALIGN)
            pick(0, 0, M, picked)
            width = BANK if (b, u) == (H_PASSES - 1, 1) else M
            for lo in range(0, M, width):
                pick(1, lo, lo + width, picked)
            return picked

        def join_pair(b, u, picked):
            for lo in range(0, M, JOIN):
                total = psum.tile([P, JOIN // P, PAIR, P], F32, name=f"total{b}{u}_{lo}", tag="total", bufs=2)
                places = [
                    (block, e, slice(lo + block * P, lo + (block + 1) * P)) for e in range(PAIR) for block in range(JOIN // P)
                ]
                for n, (block, e, cols) in enumerate(places):
                    nc.tensor.matmul(
                        total[:, block, e, :],
                        room_t[b][:, PAIR * u + e, cols],
                        ident[:],
                        start=(n == 0),
                        stop=False,
                        is_transpose=True,
                    )
                for n, (block, e, cols) in enumerate(places):
                    nc.tensor.matmul(
                        total[:, block, e, :],
                        picked[:, e, cols],
                        ident[:],
                        start=False,
                        stop=(n == len(places) - 1),
                        is_transpose=True,
                    )
                if (b, lo) == (H_PASSES - 1, M - JOIN):
                    turned = ring.tile(
                        [P, PAIR * JOIN], BF16, name="turned_last", tag="after_last_reader", align_bytes=MX_ALIGN
                    )
                else:
                    turned = ring.tile([P, PAIR * JOIN], BF16, name=f"turned{b}{u}_{lo}", tag="turned", bufs=3)
                nc.scalar.copy(
                    turned[:].rearrange("m (block p e) -> m block p e", block=JOIN // P, e=PAIR),
                    total[:].rearrange("m block e p -> m block p e"),
                )
                back = psum.tile([P, JOIN], F32, name=f"back{b}{u}_{lo}", tag="back", bufs=2)
                for block in range(JOIN // P):
                    cols = slice(block * P, (block + 1) * P)
                    nc.tensor.transpose(back[:, cols], turned[:].bitcast(F32)[:, cols], ident[:])
                words = z_bf(b, lo, lo + JOIN).bitcast(F32).rearrange("p (m u) -> p m u", u=PACK // PAIR)
                nc.scalar.copy(words[:, :, u], back[:])

        def quantise_z(b, lo, hi):
            nc.vector.quantize_mx(z_codes[b][:, lo:hi].bitcast(FP8X4), z_planes[b][:, lo:hi], z_bf(b, lo, hi))

        picked = pick_pair(0, 0, "after_last_reader")
        put_pair(0, 1)
        join_pair(0, 0, picked)
        codes1 = ring.tile([P, K_PASSES, PASS], U32, name="codes1", tag="after_last_reader", align_bytes=MX_ALIGN)
        quantise_w1(1, codes1)
        respond_pair(1, 0)
        picked = pick_pair(0, 1, "after_w1")
        put_pair(1, 0)
        respond_pair(1, 1)
        join_pair(0, 1, picked)
        quantise_z(0, 0, M)
        picked = pick_pair(1, 0, "after_z0")
        put_pair(1, 1)
        join_pair(1, 0, picked)

        def multiply(b, banks, lo, hi):
            for acc, chunks in banks:
                steps = [(n, c, m0) for n, c in enumerate(chunks) for m0 in range(lo, hi, P)]
                for step in steps:
                    n, c, m0 = step
                    nc.tensor.matmul_mx(
                        acc[:, n, m0 - lo : m0 - lo + P],
                        lhsT=w4_codes[:, b, 2 * c * P : 2 * (c + 1) * P].bitcast(FP4X4),
                        lhsT_scale=w4_planes[:, b, c * P : (c + 1) * P],
                        rhs=z_codes[b][:, m0 : m0 + P].bitcast(FP8X4),
                        rhs_scale=z_planes[b][:, m0 : m0 + P],
                        start=(b == 0 and step == steps[0]),
                        stop=(b == H_PASSES - 1 and step == steps[-1]),
                    )

        spans, banks, taken = [], {}, 0
        bank_tags = [("acc", 4)] * 4 + [("total", 2)] * 2 + [("back", 2)] * 2
        for width in LAST_WIDTHS:
            lo = spans[-1][1] if spans else 0
            spans.append((lo, lo + width))
            per_bank = BANK // width
            banks[lo] = []
            for c in range(0, N // P, per_bank):
                chunks = range(c, min(c + per_bank, N // P))
                tag, bufs = bank_tags[taken]
                taken = taken + 1
                acc = psum.tile([P, len(chunks), width], F32, name=f"out{lo}_{c}", tag=tag, bufs=bufs)
                banks[lo].append((acc, chunks))
            multiply(0, banks[lo], lo, lo + width)

        picked = pick_pair(1, 1, "after_last_reader")

        def add_room(lo, hi):
            nc.vector.tensor_tensor(
                z_bf(1, lo, hi).rearrange("p (m k u e) -> p u m e k", k=2, u=PACK // PAIR, e=PAIR)[:, 1, :, :, :],
                picked[:, :, lo:hi].rearrange("p e (m k) -> p m e k", k=2),
                room_t[1][:, PAIR:PACK, lo:hi].rearrange("p e (m k) -> p m e k", k=2),
                ADD,
            )

        def conclude(lo, hi):
            quantise_z(1, lo, hi)
            multiply(1, banks[lo], lo, hi)
            result = keep.tile([P, N // P, hi - lo], F32, name=f"result{lo}")
            for acc, chunks in banks[lo]:
                for n, c in enumerate(chunks):
                    if hi == M:
                        nc.vector.tensor_scalar(result[:, c, :], acc[:, n, :], b2_t[:, c : c + 1], None, ADD)
                    else:
                        nc.scalar.activation(result[:, c, :], acc[:, n, :], ACT.Identity, bias=b2_t[:, c : c + 1])
            nc.sync.dma_start(out[:, lo:hi].rearrange("(c p) m -> p c m", p=P), result[:])

        add_room(*spans[0])
        for before, span in zip(spans, spans[1:]):
            add_room(*span)
            conclude(*before)
        conclude(*spans[-1])
